import numpy as np
import ml_dtypes


def mxq(x, axis, fmt="e4m3"):
    dtype, down = {"e4m3": (ml_dtypes.float8_e4m3fn, 7), "e5m2": (ml_dtypes.float8_e5m2, 14)}[fmt]
    v = np.moveaxis(np.asarray(x, np.float32).astype(ml_dtypes.bfloat16).astype(np.float64), axis, -1)
    blocks = v.reshape(v.shape[:-1] + (-1, 32))
    amax = np.abs(blocks).max(-1, keepdims=True)
    byte = np.maximum(np.where(amax > 0, np.frexp(amax)[1] - 1 + 127, 0) - down, 1)
    scale = np.exp2(byte - 127.0)
    codes = (blocks / scale).astype(np.float32).astype(dtype).astype(np.float64)
    return np.moveaxis((codes * scale).reshape(v.shape), -1, axis)


WIDE = False


def mx_kscale(k):
    if not WIDE:
        return np.ones(k)
    levels = np.array([10, -10, 5, -5, 0])
    if k % 512:
        return np.exp2(np.random.permutation(np.resize(levels, k // 32))).repeat(32)
    a = np.empty((k // 512, 16))
    for p in range(k // 512):
        a[p, :8] = np.random.permutation(np.resize(levels, 8))
        for g in range(8):
            far = levels[np.abs(levels - a[p, g]) >= 10]
            a[p, g + 8] = far[np.random.randint(len(far))]
    return np.exp2(a.ravel()).repeat(32)


def f64(x):
    return np.asarray(x).astype(np.float64)


def striped(idx):
    return np.tile(idx.reshape(-1, 16).T, (8, 1)).astype(np.uint16)


def unstriped(offs):
    return offs[:16].T.reshape(-1).astype(np.int64)


E2M1 = np.array([0.0, 0.5, 1.0, 1.5, 2.0, 3.0, 4.0, 6.0, -0.0, -0.5, -1.0, -1.5, -2.0, -3.0, -4.0, -6.0])


def pack_weight(w, fmt):
    k, n = w.shape
    w = f64(np.asarray(w, np.float32).astype(ml_dtypes.bfloat16)).reshape(k // 32, 32, n)
    amax = np.abs(w).max(1)
    if fmt == "e4m3":
        byte = np.frexp(amax)[1] - 1 + 127 - 7
    else:
        mant, ex = np.frexp(amax / 6.0)
        byte = np.where(mant > 0.5, ex, ex - 1) + 127
    byte = np.clip(np.where(amax > 0, byte, 1), 1, 254)
    scaled = (w * np.exp2(127.0 - byte)[:, None, :]).reshape(k, n).astype(np.float32)
    by_word = np.ascontiguousarray(scaled.reshape(k // 512, 128, 4, n).transpose(0, 1, 3, 2))
    if fmt == "e4m3":
        words = by_word.astype(ml_dtypes.float8_e4m3fn).view(np.uint8)
    else:
        c = by_word.astype(ml_dtypes.float4_e2m1fn).view(np.uint8) & 0xF
        words = (c[..., 0::2] | (c[..., 1::2] << 4)).reshape(k // 512, 128, 2 * n)
    return np.ascontiguousarray(words), np.ascontiguousarray(byte.astype(np.uint8).reshape(k // 512, 16, n))


def unpack_weight(words, scales, fmt):
    g, _, n = scales.shape
    words = np.ascontiguousarray(words).reshape(g, 128, n, -1)
    if fmt == "e4m3":
        vals = words.view(ml_dtypes.float8_e4m3fn).astype(np.float64)
    else:
        nib = np.empty((g, 128, n, 4), np.uint8)
        nib[..., 0::2] = words & 0xF
        nib[..., 1::2] = words >> 4
        vals = E2M1[nib]
    vals = vals * np.repeat(np.exp2(scales.astype(np.float64) - 127.0), 8, axis=1)[..., None]
    return vals.transpose(0, 1, 3, 2).reshape(g * 512, n)


def gelu(v):
    return 0.5 * v * (1.0 + np.tanh(np.sqrt(2.0 / np.pi) * (v + 0.044715 * v**3)))


K, H, N, T, S, P, P2 = 1024, 1024, 512, 4096, 2048, 1024, 512

def setup_inputs():
    n = np.random.standard_normal
    s = mx_kscale(K)[:, None]
    u = mx_kscale(H)[:, None]
    tab_words, tab_scales = pack_weight(n((K, T)) * s, "e4m3")
    w4_words, w4_scales = pack_weight(1.3 * n((K, H)) / np.sqrt(K) / s, "e2m1")
    return {
        "tab_words": tab_words, "tab_scales": tab_scales,
        "offs": striped(np.random.permutation(T)[:S]),
        "pos1": striped(np.random.permutation(S)[:P]),
        "pos2": striped(np.random.permutation(S)[:P]),
        "pos3": striped(np.random.permutation(P)[:P2]),
        "pos4": striped(np.random.permutation(S)[:P2]),
        "w4_words": w4_words, "w4_scales": w4_scales,
        "b1": (0.5 * n(H)).astype(np.float32),
        "gain": (np.exp(0.3 * n(H)) * u[:, 0]).astype(np.float32),
        "w2": (1.5 * n((H, N)) / np.sqrt(H) / u).astype(np.float32),
        "b2": (0.5 * n(N)).astype(np.float32),
    }

def reference(tab_words, tab_scales, offs, pos1, pos2, pos3, pos4, w4_words, w4_scales, b1, gain, w2, b2):
    v = unpack_weight(tab_words, tab_scales, "e4m3")[:, unstriped(offs)]
    w4 = unpack_weight(w4_words, w4_scales, "e2m1")
    x = (w4.T @ v) + f64(b1)[:, None]
    h = 0.5 * x * (1.0 + np.tanh(np.sqrt(2.0 / np.pi) * (x + 0.044715 * x ** 3)))
    a1 = f64(gain)[:, None] * np.maximum(h[:, unstriped(pos1)], h[:, unstriped(pos2)])
    a2 = a1[:, unstriped(pos3)] * np.tanh(h[:, unstriped(pos4)])
    a2q = mxq(a2, 0, "e4m3")
    w2q = mxq(f64(w2), 0, "e4m3")
    return (w2q.T @ a2q) + f64(b2)[:, None]

@@ -1,0 +1,230 @@
+from contextlib import ExitStack
+
+import concourse.mybir as mybir
+from concourse.masks import make_identity
+
+K, H, N, T, S, PAIRS, KEPT = 1024, 1024, 512, 4096, 2048, 1024, 512
+FLOPS = 2 * K * H * S + 2 * H * N * KEPT
+
+F32 = mybir.dt.float32
+BF16 = mybir.dt.bfloat16
+I32 = mybir.dt.int32
+U32 = mybir.dt.uint32
+U16 = mybir.dt.uint16
+U8 = mybir.dt.uint8
+FP8X4 = mybir.dt.float8_e4m3fn_x4
+FP4X4 = mybir.dt.float4_e2m1fn_x4
+ACT = mybir.ActivationFunctionType
+ALU = mybir.AluOpType
+
+P = 128
+PASSES = 2
+PACK = 4
+SLICES = 8
+BANK = 512
+CHUNKS = S // BANK
+HALF = KEPT // 2
+
+
+def tile_list_juror_pair_leanings_kernel(
+    tc, tab_words, tab_scales, offs, pos1, pos2, pos3, pos4, w4_words, w4_scales, b1, gain, w2, b2, out
+):
+    nc = tc.nc
+    with ExitStack() as ctx:
+        keep = ctx.enter_context(tc.tile_pool(name="keep", bufs=1))
+        two = ctx.enter_context(tc.tile_pool(name="two", bufs=2))
+        three = ctx.enter_context(tc.tile_pool(name="three", bufs=3))
+        ps_h = ctx.enter_context(tc.psum_pool(name="ps_h", bufs=4))
+        ps_o = ctx.enter_context(tc.psum_pool(name="ps_o", bufs=1))
+
+        offs_sb = keep.tile([P, S // 16], U16, name="offs_sb")
+        nc.sync.dma_start(offs_sb[:], offs)
+        tscale = keep.tile([P, T], U8, name="tscale", align_bytes=64)
+        nc.sync.dma_start(tscale[96:128, :].bitcast(I32), tab_scales.rearrange("a q t -> (a q) t").bitcast(I32))
+        nc.vector.memset(tscale[0:96, :].bitcast(I32), 0)
+        planes = keep.tile([P, PASSES * S], U8, name="planes", align_bytes=64)
+        nc.vector.memset(planes[:].bitcast(I32), 0)
+
+        tab0 = keep.tile([P, T], I32, name="tab0", tag="tab0_then_w2", align_bytes=64)
+        nc.sync.dma_start(tab0[:], tab_words[0].rearrange("p n t -> p (n t)").bitcast(I32))
+        w4_raw = keep.tile([P, PASSES, 2 * H // 4], I32, name="w4_raw", align_bytes=64)
+        nc.sync.dma_start(w4_raw[:], w4_words.rearrange("a p c -> p a c").bitcast(I32))
+        pos_sb = []
+        for name, lst, n in (("pos4", pos4, KEPT), ("pos2", pos2, PAIRS), ("pos1", pos1, PAIRS), ("pos3", pos3, KEPT)):
+            lst_sb = keep.tile([P, n // 16], U16, name=name + "_sb")
+            nc.sync.dma_start(lst_sb[:], lst)
+            pos_sb.append(lst_sb)
+        pos4_sb, pos2_sb, pos1_sb, pos3_sb = pos_sb
+        tab1 = keep.tile([P, T], I32, name="tab1", align_bytes=64)
+        nc.sync.dma_start(tab1[:], tab_words[1].rearrange("p n t -> p (n t)").bitcast(I32))
+        tab = (tab0, tab1)
+
+        ident = keep.tile([P, P], F32, name="ident")
+        make_identity(nc, ident[:])
+        w4s_raw = keep.tile([P, PASSES, H // 4], I32, name="w4s_raw", align_bytes=64)
+        nc.gpsimd.memset(w4s_raw[:], 0)
+        for q in range(4):
+            nc.gpsimd.dma_start(
+                w4s_raw[32 * q : 32 * q + 4, :, :],
+                w4_scales[:, 4 * q : 4 * q + 4, :].rearrange("a r c -> r a c").bitcast(I32),
+            )
+        rows = keep.tile([P, P], F32, name="rows")
+        nc.gpsimd.memset(rows[:], 0.0)
+        for first, vec in ((0, b1), (SLICES, gain)):
+            nc.gpsimd.dma_start(
+                rows[first : first + SLICES, :].rearrange("u (g i) -> u g i", i=8),
+                vec.rearrange("(g u i) -> u g i", u=SLICES, i=8),
+            )
+        nc.gpsimd.dma_start(rows[2 * SLICES : 2 * SLICES + 4, :], b2.rearrange("(c p) -> c p", p=P))
+        cols_ps = ps_h.tile([P, P], F32, name="cols_ps", tag="bank")
+        nc.tensor.transpose(cols_ps[:], rows[:], ident[:])
+        cols = keep.tile([P, 2 * SLICES + 4], F32, name="cols")
+        nc.scalar.copy(cols[:], cols_ps[:, 0 : 2 * SLICES + 4])
+
+        gscale = keep.tile([P, S], U8, name="gscale", align_bytes=64)
+        nc.vector.tensor_copy(gscale[:], tscale[:].indirect(offs_sb[:]))
+        for a in range(PASSES):
+            for q in range(4):
+                src = 96 + 16 * a + 4 * q
+                nc.scalar.dma_start(
+                    planes[32 * q : 32 * q + 4, a * S : (a + 1) * S].bitcast(I32), gscale[src : src + 4, :].bitcast(I32)
+                )
+        codes = [keep.tile([P, S], U32, name="codes%d" % a, align_bytes=64) for a in range(PASSES)]
+
+        def gather_words(a, c):
+            nc.vector.tensor_copy(
+                codes[a][:, c * BANK : (c + 1) * BANK],
+                tab[a][:].bitcast(U32).indirect(offs_sb[:, c * BANK // 16 : (c + 1) * BANK // 16]),
+            )
+
+        for c in range(CHUNKS):
+            gather_words(0, c)
+
+        w4 = keep.tile([P, PASSES * 2 * H], U8, name="w4", align_bytes=64)
+        nc.vector.tensor_copy(
+            w4[:].bitcast(I32).rearrange("p (a u g w) -> p a u g w", a=PASSES, u=SLICES, w=4),
+            w4_raw[:].rearrange("p a (g u w) -> p a u g w", u=SLICES, w=4),
+        )
+        w4s = keep.tile([P, PASSES * H], U8, name="w4s", align_bytes=64)
+        nc.vector.tensor_copy(
+            w4s[:].bitcast(I32).rearrange("p (a u g w) -> p a u g w", a=PASSES, u=SLICES, w=2),
+            w4s_raw[:].rearrange("p a (g u w) -> p a u g w", u=SLICES, w=2),
+        )
+        for c in range(CHUNKS):
+            gather_words(1, c)
+
+        w2_raw = keep.tile([P, SLICES, N], F32, name="w2_raw", tag="tab0_then_w2", align_bytes=64)
+        w2_rows = w2.rearrange("(g u i) n -> u g i n", u=SLICES, i=8)
+        for u in range(SLICES):
+            nc.sync.dma_start(w2_raw[:, u, :], w2_rows[u])
+
+        def first_stage(u):
+            h = three.tile([P, S], F32, name="h")
+            for c in range(CHUNKS):
+                bank = ps_h.tile([P, BANK], F32, name="bank", tag="bank")
+                for a in range(PASSES):
+                    col = (a * SLICES + u) * P
+                    nc.tensor.matmul_mx(
+                        out=bank[:],
+                        lhsT=w4[:, 2 * col : 2 * (col + P)].bitcast(FP4X4),
+                        lhsT_scale=w4s[:, col : col + P],
+                        rhs=codes[a][:, c * BANK : (c + 1) * BANK].bitcast(FP8X4),
+                        rhs_scale=planes[:, a * S + c * BANK : a * S + (c + 1) * BANK],
+                        start=(a == 0),
+                        stop=(a == PASSES - 1),
+                    )
+                nc.scalar.activation(
+                    h[:, c * BANK : (c + 1) * BANK], bank[:], ACT.Gelu_apprx_tanh, bias=cols[:, u : u + 1]
+                )
+            return h
+
+        def weave(copy, dst, src):
+            copy(
+                dst.rearrange("p (c i) t -> p c t i", i=4),
+                src.rearrange("p t (c i) -> p c t i", i=4),
+            )
+
+        def quantize(codes_ap, scales_ap, woven):
+            nc.vector.quantize_mx(
+                out=codes_ap.bitcast(FP8X4), scales=scales_ap, in_=woven[:].rearrange("p c t -> p (c t)")
+            )
+
+        w2_woven = [keep.tile([P, N, PACK], BF16, name="w2_woven%d" % b, align_bytes=64) for b in range(PASSES)]
+        w2_codes = keep.tile([P, PASSES * N], U32, name="w2_codes", align_bytes=64)
+        w2_scales = keep.tile([P, PASSES * N], U8, name="w2_scales", align_bytes=64)
+        a2 = [keep.tile([P, PACK, KEPT], F32, name="a2_%d" % b, align_bytes=64) for b in range(PASSES)]
+        a2_codes = keep.tile([P, PASSES * KEPT], U32, name="a2_codes", align_bytes=64)
+        a2_scales = keep.tile([P, PASSES * KEPT], U8, name="a2_scales", align_bytes=64)
+        acc = [ps_o.tile([P, KEPT], F32, name="acc%d" % c) for c in range(N // P)]
+
+        def second_stage(b, lo, hi, start, stop):
+            for c in range(N // P):
+                nc.tensor.matmul_mx(
+                    out=acc[c][:, lo:hi],
+                    lhsT=w2_codes[:, b * N + c * P : b * N + (c + 1) * P].bitcast(FP8X4),
+                    lhsT_scale=w2_scales[:, b * N + c * P : b * N + (c + 1) * P],
+                    rhs=a2_codes[:, b * KEPT + lo : b * KEPT + hi].bitcast(FP8X4),
+                    rhs_scale=a2_scales[:, b * KEPT + lo : b * KEPT + hi],
+                    start=start,
+                    stop=stop,
+                )
+
+        def kept_pairs(u, a1, factor, lo, hi):
+            nc.vector.tensor_tensor(
+                a2[u // PACK][:, u % PACK, lo:hi],
+                a1[:].indirect(pos3_sb[:, lo // 16 : hi // 16]),
+                factor[:, lo:hi],
+                ALU.mult,
+            )
+
+        hs = [first_stage(0), first_stage(1)]
+        a1s, factors = [], []
+        a2_woven0 = keep.tile([P, KEPT, PACK], BF16, name="a2_woven0", align_bytes=64)
+        for u in range(SLICES):
+            h = hs[u]
+            alt = two.tile([P, KEPT], F32, name="alt")
+            nc.vector.tensor_copy(alt[:], h[:].indirect(pos4_sb[:]))
+            alt_tanh = two.tile([P, KEPT], F32, name="alt_tanh")
+            nc.scalar.activation(alt_tanh[:], alt[:], ACT.Tanh)
+            factor = three.tile([P, KEPT], F32, name="factor")
+            nc.scalar.activation(factor[:], alt_tanh[:], ACT.Copy, scale=cols[:, SLICES + u : SLICES + u + 1])
+            factors.append(factor)
+            second = two.tile([P, PAIRS], F32, name="second")
+            nc.vector.tensor_copy(second[:], h[:].indirect(pos2_sb[:]))
+            first = two.tile([P, PAIRS], F32, name="first")
+            a1 = two.tile([P, PAIRS], F32, name="a1")
+            nc.vector.tensor_copy(first[:], h[:].indirect(pos1_sb[:]))
+            if u + 2 < SLICES:
+                hs.append(first_stage(u + 2))
+            if u > 0:
+                kept_pairs(u - 1, a1s[u - 1], factors[u - 1], 0, KEPT)
+            nc.vector.tensor_tensor(a1[:], first[:], second[:], ALU.max)
+            a1s.append(a1)
+            if u < 2 * PASSES:
+                b, lo = u // 2, (u % 2) * HALF
+                weave(nc.scalar.copy, w2_woven[b][:, lo : lo + HALF, :], w2_raw[:, b * PACK : (b + 1) * PACK, lo : lo + HALF])
+            if u == PACK:
+                weave(nc.scalar.copy, a2_woven0[:], a2[0][:])
+                for b in range(PASSES):
+                    quantize(w2_codes[:, b * N : (b + 1) * N], w2_scales[:, b * N : (b + 1) * N], w2_woven[b])
+            if u == PACK + 1:
+                quantize(a2_codes[:, 0:KEPT], a2_scales[:, 0:KEPT], a2_woven0)
+                second_stage(0, 0, KEPT, True, False)
+
+        halves = [keep.tile([P, HALF, PACK], BF16, name="a2_half%d" % j, align_bytes=64) for j in range(2)]
+        last = SLICES - 1
+        for j, copy in enumerate((nc.scalar.copy, nc.vector.tensor_copy)):
+            kept_pairs(last, a1s[last], factors[last], j * HALF, (j + 1) * HALF)
+            weave(copy, halves[j][:], a2[1][:, :, j * HALF : (j + 1) * HALF])
+        for j in range(2):
+            lo, hi = j * HALF, (j + 1) * HALF
+            quantize(a2_codes[:, KEPT + lo : KEPT + hi], a2_scales[:, KEPT + lo : KEPT + hi], halves[j])
+            second_stage(1, lo, hi, False, j == 1)
+        for c in range(N // P):
+            res = keep.tile([P, KEPT], F32, name="res%d" % c)
+            bias = cols[:, 2 * SLICES + c : 2 * SLICES + c + 1]
+            if c % 2 == 0:
+                nc.scalar.activation(res[:], acc[c][:], ACT.Identity, bias=bias)
+            else:
+                nc.vector.tensor_scalar_add(res[:], acc[c][:], bias)
+            nc.sync.dma_start(out[c * P : (c + 1) * P, :], res[:])

@@ -37,6 +37,8 @@ def tile_list_juror_pair_leanings_kernel(
         ps_h = ctx.enter_context(tc.psum_pool(name="ps_h", bufs=4))
         ps_o = ctx.enter_context(tc.psum_pool(name="ps_o", bufs=1))
 
+        rows = keep.tile([P, P], F32, name="rows")
+        nc.gpsimd.memset(rows[:], 0.0)
         offs_sb = keep.tile([P, S // 16], U16, name="offs_sb")
         nc.sync.dma_start(offs_sb[:], offs)
         tscale = keep.tile([P, T], U8, name="tscale", align_bytes=64)
@@ -49,18 +51,26 @@ def tile_list_juror_pair_leanings_kernel(
         nc.sync.dma_start(tab0[:], tab_words[0].rearrange("p n t -> p (n t)").bitcast(I32))
         w4_raw = keep.tile([P, PASSES, 2 * H // 4], I32, name="w4_raw", align_bytes=64)
         nc.sync.dma_start(w4_raw[:], w4_words.rearrange("a p c -> p a c").bitcast(I32))
-        pos_sb = []
-        for name, lst, n in (("pos4", pos4, KEPT), ("pos2", pos2, PAIRS), ("pos1", pos1, PAIRS), ("pos3", pos3, KEPT)):
-            lst_sb = keep.tile([P, n // 16], U16, name=name + "_sb")
+        for first, vec in ((0, b1), (SLICES, gain)):
+            nc.sync.dma_start(
+                rows[first : first + SLICES, :].rearrange("u (g i) -> u g i", i=8),
+                vec.rearrange("(g u i) -> u g i", u=SLICES, i=8),
+            )
+        nc.sync.dma_start(rows[2 * SLICES : 2 * SLICES + 4, :], b2.rearrange("(c p) -> c p", p=P))
+
+        def load_list(name, lst, n):
+            lst_sb = keep.tile([P, n // 16], U16, name=name)
             nc.sync.dma_start(lst_sb[:], lst)
-            pos_sb.append(lst_sb)
-        pos4_sb, pos2_sb, pos1_sb, pos3_sb = pos_sb
+            return lst_sb
+
+        pos4_sb = load_list("pos4_sb", pos4, KEPT)
         tab1 = keep.tile([P, T], I32, name="tab1", align_bytes=64)
         nc.sync.dma_start(tab1[:], tab_words[1].rearrange("p n t -> p (n t)").bitcast(I32))
         tab = (tab0, tab1)
+        pos2_sb = load_list("pos2_sb", pos2, PAIRS)
+        pos1_sb = load_list("pos1_sb", pos1, PAIRS)
+        pos3_sb = load_list("pos3_sb", pos3, KEPT)
 
-        ident = keep.tile([P, P], F32, name="ident")
-        make_identity(nc, ident[:])
         w4s_raw = keep.tile([P, PASSES, H // 4], I32, name="w4s_raw", align_bytes=64)
         nc.gpsimd.memset(w4s_raw[:], 0)
         for q in range(4):
@@ -68,14 +78,8 @@ def tile_list_juror_pair_leanings_kernel(
                 w4s_raw[32 * q : 32 * q + 4, :, :],
                 w4_scales[:, 4 * q : 4 * q + 4, :].rearrange("a r c -> r a c").bitcast(I32),
             )
-        rows = keep.tile([P, P], F32, name="rows")
-        nc.gpsimd.memset(rows[:], 0.0)
-        for first, vec in ((0, b1), (SLICES, gain)):
-            nc.gpsimd.dma_start(
-                rows[first : first + SLICES, :].rearrange("u (g i) -> u g i", i=8),
-                vec.rearrange("(g u i) -> u g i", u=SLICES, i=8),
-            )
-        nc.gpsimd.dma_start(rows[2 * SLICES : 2 * SLICES + 4, :], b2.rearrange("(c p) -> c p", p=P))
+        ident = keep.tile([P, P], F32, name="ident")
+        make_identity(nc, ident[:])
         cols_ps = ps_h.tile([P, P], F32, name="cols_ps", tag="bank")
         nc.tensor.transpose(cols_ps[:], rows[:], ident[:])
         cols = keep.tile([P, 2 * SLICES + 4], F32, name="cols")
@@ -189,16 +193,24 @@ def tile_list_juror_pair_leanings_kernel(
             factor = three.tile([P, KEPT], F32, name="factor")
             nc.scalar.activation(factor[:], alt_tanh[:], ACT.Copy, scale=cols[:, SLICES + u : SLICES + u + 1])
             factors.append(factor)
-            second = two.tile([P, PAIRS], F32, name="second")
+            second = three.tile([P, PAIRS], F32, name="second")
             nc.vector.tensor_copy(second[:], h[:].indirect(pos2_sb[:]))
             first = two.tile([P, PAIRS], F32, name="first")
             a1 = two.tile([P, PAIRS], F32, name="a1")
-            nc.vector.tensor_copy(first[:], h[:].indirect(pos1_sb[:]))
+            if u < SLICES - 1:
+                nc.vector.tensor_tensor(first[:], h[:].indirect(pos1_sb[:]), second[:], ALU.subtract)
+            else:
+                nc.vector.tensor_copy(first[:], h[:].indirect(pos1_sb[:]))
             if u + 2 < SLICES:
                 hs.append(first_stage(u + 2))
+            if u < SLICES - 1:
+                excess = two.tile([P, PAIRS], F32, name="excess")
+                nc.scalar.activation(excess[:], first[:], ACT.Relu)
+                nc.gpsimd.tensor_tensor(a1[:], excess[:], second[:], ALU.add)
             if u > 0:
                 kept_pairs(u - 1, a1s[u - 1], factors[u - 1], 0, KEPT)
-            nc.vector.tensor_tensor(a1[:], first[:], second[:], ALU.max)
+            if u == SLICES - 1:
+                nc.vector.tensor_tensor(a1[:], first[:], second[:], ALU.max)
             a1s.append(a1)
             if u < 2 * PASSES:
                 b, lo = u // 2, (u % 2) * HALF

@@ -24,6 +24,7 @@ SLICES = 8
 BANK = 512
 CHUNKS = S // BANK
 HALF = KEPT // 2
+ROW0 = P - (2 * SLICES + N // P)
 
 
 def tile_list_juror_pair_leanings_kernel(
@@ -34,11 +35,12 @@ def tile_list_juror_pair_leanings_kernel(
         keep = ctx.enter_context(tc.tile_pool(name="keep", bufs=1))
         two = ctx.enter_context(tc.tile_pool(name="two", bufs=2))
         three = ctx.enter_context(tc.tile_pool(name="three", bufs=3))
+        four = ctx.enter_context(tc.tile_pool(name="four", bufs=4))
         ps_h = ctx.enter_context(tc.psum_pool(name="ps_h", bufs=4))
         ps_o = ctx.enter_context(tc.psum_pool(name="ps_o", bufs=1))
 
         rows = keep.tile([P, P], F32, name="rows")
-        nc.gpsimd.memset(rows[:], 0.0)
+        nc.gpsimd.memset(rows[0:ROW0, :], 0.0)
         offs_sb = keep.tile([P, S // 16], U16, name="offs_sb")
         nc.sync.dma_start(offs_sb[:], offs)
         tscale = keep.tile([P, T], U8, name="tscale", align_bytes=64)
@@ -47,16 +49,16 @@ def tile_list_juror_pair_leanings_kernel(
         planes = keep.tile([P, PASSES * S], U8, name="planes", align_bytes=64)
         nc.vector.memset(planes[:].bitcast(I32), 0)
 
-        tab0 = keep.tile([P, T], I32, name="tab0", tag="tab0_then_w2", align_bytes=64)
+        tab0 = keep.tile([P, T], I32, name="tab0", align_bytes=64)
         nc.sync.dma_start(tab0[:], tab_words[0].rearrange("p n t -> p (n t)").bitcast(I32))
         w4_raw = keep.tile([P, PASSES, 2 * H // 4], I32, name="w4_raw", align_bytes=64)
         nc.sync.dma_start(w4_raw[:], w4_words.rearrange("a p c -> p a c").bitcast(I32))
-        for first, vec in ((0, b1), (SLICES, gain)):
+        for first, vec in ((ROW0, b1), (ROW0 + SLICES, gain)):
             nc.sync.dma_start(
                 rows[first : first + SLICES, :].rearrange("u (g i) -> u g i", i=8),
                 vec.rearrange("(g u i) -> u g i", u=SLICES, i=8),
             )
-        nc.sync.dma_start(rows[2 * SLICES : 2 * SLICES + 4, :], b2.rearrange("(c p) -> c p", p=P))
+        nc.sync.dma_start(rows[ROW0 + 2 * SLICES :, :], b2.rearrange("(c p) -> c p", p=P))
 
         def load_list(name, lst, n):
             lst_sb = keep.tile([P, n // 16], U16, name=name)
@@ -64,7 +66,7 @@ def tile_list_juror_pair_leanings_kernel(
             return lst_sb
 
         pos4_sb = load_list("pos4_sb", pos4, KEPT)
-        tab1 = keep.tile([P, T], I32, name="tab1", align_bytes=64)
+        tab1 = keep.tile([P, T], I32, name="tab1", tag="tab1_then_w2", align_bytes=64)
         nc.sync.dma_start(tab1[:], tab_words[1].rearrange("p n t -> p (n t)").bitcast(I32))
         tab = (tab0, tab1)
         pos2_sb = load_list("pos2_sb", pos2, PAIRS)
@@ -83,7 +85,6 @@ def tile_list_juror_pair_leanings_kernel(
         cols_ps = ps_h.tile([P, P], F32, name="cols_ps", tag="bank")
         nc.tensor.transpose(cols_ps[:], rows[:], ident[:])
         cols = keep.tile([P, 2 * SLICES + 4], F32, name="cols")
-        nc.scalar.copy(cols[:], cols_ps[:, 0 : 2 * SLICES + 4])
 
         gscale = keep.tile([P, S], U8, name="gscale", align_bytes=64)
         nc.vector.tensor_copy(gscale[:], tscale[:].indirect(offs_sb[:]))
@@ -95,51 +96,51 @@ def tile_list_juror_pair_leanings_kernel(
                 )
         codes = [keep.tile([P, S], U32, name="codes%d" % a, align_bytes=64) for a in range(PASSES)]
 
-        def gather_words(a, c):
-            nc.vector.tensor_copy(
-                codes[a][:, c * BANK : (c + 1) * BANK],
-                tab[a][:].bitcast(U32).indirect(offs_sb[:, c * BANK // 16 : (c + 1) * BANK // 16]),
-            )
+        def gather_words(a, lo, hi):
+            nc.vector.tensor_copy(codes[a][:, lo:hi], tab[a][:].bitcast(U32).indirect(offs_sb[:, lo // 16 : hi // 16]))
 
         for c in range(CHUNKS):
-            gather_words(0, c)
+            gather_words(0, c * BANK, (c + 1) * BANK)
 
+        nc.vector.tensor_copy(cols[:], cols_ps[:, ROW0:])
         w4 = keep.tile([P, PASSES * 2 * H], U8, name="w4", align_bytes=64)
-        nc.vector.tensor_copy(
-            w4[:].bitcast(I32).rearrange("p (a u g w) -> p a u g w", a=PASSES, u=SLICES, w=4),
-            w4_raw[:].rearrange("p a (g u w) -> p a u g w", u=SLICES, w=4),
-        )
         w4s = keep.tile([P, PASSES * H], U8, name="w4s", align_bytes=64)
-        nc.vector.tensor_copy(
-            w4s[:].bitcast(I32).rearrange("p (a u g w) -> p a u g w", a=PASSES, u=SLICES, w=2),
-            w4s_raw[:].rearrange("p a (g u w) -> p a u g w", u=SLICES, w=2),
-        )
+        for a in range(PASSES):
+            nc.gpsimd.tensor_copy(
+                w4s[:, a * H : (a + 1) * H].bitcast(I32).rearrange("p (u g w) -> p u g w", u=SLICES, w=2),
+                w4s_raw[:, a, :].rearrange("p (g u w) -> p u g w", u=SLICES, w=2),
+            )
+            nc.gpsimd.tensor_copy(
+                w4[:, a * 2 * H : (a + 1) * 2 * H].bitcast(I32).rearrange("p (u g w) -> p u g w", u=SLICES, w=4),
+                w4_raw[:, a, :].rearrange("p (g u w) -> p u g w", u=SLICES, w=4),
+            )
         for c in range(CHUNKS):
-            gather_words(1, c)
+            gather_words(1, c * BANK, (c + 1) * BANK)
 
-        w2_raw = keep.tile([P, SLICES, N], F32, name="w2_raw", tag="tab0_then_w2", align_bytes=64)
+        w2_raw = keep.tile([P, SLICES, N], F32, name="w2_raw", tag="tab1_then_w2", align_bytes=64)
         w2_rows = w2.rearrange("(g u i) n -> u g i n", u=SLICES, i=8)
         for u in range(SLICES):
             nc.sync.dma_start(w2_raw[:, u, :], w2_rows[u])
 
         def first_stage(u):
             h = three.tile([P, S], F32, name="h")
-            for c in range(CHUNKS):
-                bank = ps_h.tile([P, BANK], F32, name="bank", tag="bank")
+            cuts = list(range(0, S + 1, BANK))
+            if u == 0:
+                cuts.insert(-1, S - BANK // 2)
+            for lo, hi in zip(cuts, cuts[1:]):
+                bank = ps_h.tile([P, hi - lo], F32, name="bank", tag="bank")
                 for a in range(PASSES):
                     col = (a * SLICES + u) * P
                     nc.tensor.matmul_mx(
                         out=bank[:],
                         lhsT=w4[:, 2 * col : 2 * (col + P)].bitcast(FP4X4),
                         lhsT_scale=w4s[:, col : col + P],
-                        rhs=codes[a][:, c * BANK : (c + 1) * BANK].bitcast(FP8X4),
-                        rhs_scale=planes[:, a * S + c * BANK : a * S + (c + 1) * BANK],
+                        rhs=codes[a][:, lo:hi].bitcast(FP8X4),
+                        rhs_scale=planes[:, a * S + lo : a * S + hi],
                         start=(a == 0),
                         stop=(a == PASSES - 1),
                     )
-                nc.scalar.activation(
-                    h[:, c * BANK : (c + 1) * BANK], bank[:], ACT.Gelu_apprx_tanh, bias=cols[:, u : u + 1]
-                )
+                nc.scalar.activation(h[:, lo:hi], bank[:], ACT.Gelu_apprx_tanh, bias=cols[:, u : u + 1])
             return h
 
         def weave(copy, dst, src):
@@ -156,30 +157,43 @@ def tile_list_juror_pair_leanings_kernel(
         w2_woven = [keep.tile([P, N, PACK], BF16, name="w2_woven%d" % b, align_bytes=64) for b in range(PASSES)]
         w2_codes = keep.tile([P, PASSES * N], U32, name="w2_codes", align_bytes=64)
         w2_scales = keep.tile([P, PASSES * N], U8, name="w2_scales", align_bytes=64)
-        a2 = [keep.tile([P, PACK, KEPT], F32, name="a2_%d" % b, align_bytes=64) for b in range(PASSES)]
+        a2_pass0 = keep.tile([P, PACK, KEPT], F32, name="a2_pass0", align_bytes=64)
+        a2_left = keep.tile([P, PACK, HALF], F32, name="a2_left", align_bytes=64)
         a2_codes = keep.tile([P, PASSES * KEPT], U32, name="a2_codes", align_bytes=64)
         a2_scales = keep.tile([P, PASSES * KEPT], U8, name="a2_scales", align_bytes=64)
-        acc = [ps_o.tile([P, KEPT], F32, name="acc%d" % c) for c in range(N // P)]
+        acc = [[ps_o.tile([P, 2, HALF], F32, name="acc%d%d" % (j, cc)) for cc in range(2)] for j in range(2)]
 
-        def second_stage(b, lo, hi, start, stop):
+        def second_stage(b, j):
             for c in range(N // P):
+                lo = b * KEPT + j * HALF
                 nc.tensor.matmul_mx(
-                    out=acc[c][:, lo:hi],
+                    out=acc[j][c // 2][:, c % 2, :],
                     lhsT=w2_codes[:, b * N + c * P : b * N + (c + 1) * P].bitcast(FP8X4),
                     lhsT_scale=w2_scales[:, b * N + c * P : b * N + (c + 1) * P],
-                    rhs=a2_codes[:, b * KEPT + lo : b * KEPT + hi].bitcast(FP8X4),
-                    rhs_scale=a2_scales[:, b * KEPT + lo : b * KEPT + hi],
-                    start=start,
-                    stop=stop,
+                    rhs=a2_codes[:, lo : lo + HALF].bitcast(FP8X4),
+                    rhs_scale=a2_scales[:, lo : lo + HALF],
+                    start=(b == 0 and c % 2 == 0),
+                    stop=(b == PASSES - 1 and c % 2 == 1),
                 )
 
-        def kept_pairs(u, a1, factor, lo, hi):
+        def kept_pairs(dst, u, lo, hi):
             nc.vector.tensor_tensor(
-                a2[u // PACK][:, u % PACK, lo:hi],
-                a1[:].indirect(pos3_sb[:, lo // 16 : hi // 16]),
-                factor[:, lo:hi],
-                ALU.mult,
+                dst[:, u % PACK, :], a1s[u][:].indirect(pos3_sb[:, lo // 16 : hi // 16]), factors[u][:, lo:hi], ALU.mult
             )
+
+        def finish(j, on_vector):
+            for cc in range(2):
+                res = keep.tile([P, 2, HALF], F32, name="res%d%d" % (j, cc))
+                for e in range(2):
+                    c = 2 * cc + e
+                    bias = cols[:, 2 * SLICES + c : 2 * SLICES + c + 1]
+                    if cc in on_vector:
+                        nc.vector.tensor_scalar_add(res[:, e, :], acc[j][cc][:, e, :], bias)
+                    else:
+                        nc.scalar.activation(res[:, e, :], acc[j][cc][:, e, :], ACT.Identity, bias=bias)
+                nc.sync.dma_start(
+                    out[2 * cc * P : 2 * (cc + 1) * P, j * HALF : (j + 1) * HALF].rearrange("(e p) n -> p e n", p=P), res[:]
+                )
 
         hs = [first_stage(0), first_stage(1)]
         a1s, factors = [], []
@@ -190,13 +204,13 @@ def tile_list_juror_pair_leanings_kernel(
             nc.vector.tensor_copy(alt[:], h[:].indirect(pos4_sb[:]))
             alt_tanh = two.tile([P, KEPT], F32, name="alt_tanh")
             nc.scalar.activation(alt_tanh[:], alt[:], ACT.Tanh)
-            factor = three.tile([P, KEPT], F32, name="factor")
+            factor = four.tile([P, KEPT], F32, name="factor")
             nc.scalar.activation(factor[:], alt_tanh[:], ACT.Copy, scale=cols[:, SLICES + u : SLICES + u + 1])
             factors.append(factor)
             second = three.tile([P, PAIRS], F32, name="second")
             nc.vector.tensor_copy(second[:], h[:].indirect(pos2_sb[:]))
-            first = two.tile([P, PAIRS], F32, name="first")
-            a1 = two.tile([P, PAIRS], F32, name="a1")
+            first = keep.tile([P, PAIRS], F32, name="first", tag="first_then_a2", align_bytes=64)
+            a1 = four.tile([P, PAIRS], F32, name="a1")
             if u < SLICES - 1:
                 nc.vector.tensor_tensor(first[:], h[:].indirect(pos1_sb[:]), second[:], ALU.subtract)
             else:
@@ -208,7 +222,10 @@ def tile_list_juror_pair_leanings_kernel(
                 nc.scalar.activation(excess[:], first[:], ACT.Relu)
                 nc.gpsimd.tensor_tensor(a1[:], excess[:], second[:], ALU.add)
             if u > 0:
-                kept_pairs(u - 1, a1s[u - 1], factors[u - 1], 0, KEPT)
+                if u - 1 < PACK:
+                    kept_pairs(a2_pass0, u - 1, 0, KEPT)
+                else:
+                    kept_pairs(a2_left, u - 1, 0, HALF)
             if u == SLICES - 1:
                 nc.vector.tensor_tensor(a1[:], first[:], second[:], ALU.max)
             a1s.append(a1)
@@ -216,27 +233,26 @@ def tile_list_juror_pair_leanings_kernel(
                 b, lo = u // 2, (u % 2) * HALF
                 weave(nc.scalar.copy, w2_woven[b][:, lo : lo + HALF, :], w2_raw[:, b * PACK : (b + 1) * PACK, lo : lo + HALF])
             if u == PACK:
-                weave(nc.scalar.copy, a2_woven0[:], a2[0][:])
+                weave(nc.scalar.copy, a2_woven0[:], a2_pass0[:])
                 for b in range(PASSES):
                     quantize(w2_codes[:, b * N : (b + 1) * N], w2_scales[:, b * N : (b + 1) * N], w2_woven[b])
             if u == PACK + 1:
                 quantize(a2_codes[:, 0:KEPT], a2_scales[:, 0:KEPT], a2_woven0)
-                second_stage(0, 0, KEPT, True, False)
+                for j in range(2):
+                    second_stage(0, j)
 
         halves = [keep.tile([P, HALF, PACK], BF16, name="a2_half%d" % j, align_bytes=64) for j in range(2)]
         last = SLICES - 1
-        for j, copy in enumerate((nc.scalar.copy, nc.vector.tensor_copy)):
-            kept_pairs(last, a1s[last], factors[last], j * HALF, (j + 1) * HALF)
-            weave(copy, halves[j][:], a2[1][:, :, j * HALF : (j + 1) * HALF])
-        for j in range(2):
-            lo, hi = j * HALF, (j + 1) * HALF
-            quantize(a2_codes[:, KEPT + lo : KEPT + hi], a2_scales[:, KEPT + lo : KEPT + hi], halves[j])
-            second_stage(1, lo, hi, False, j == 1)
-        for c in range(N // P):
-            res = keep.tile([P, KEPT], F32, name="res%d" % c)
-            bias = cols[:, 2 * SLICES + c : 2 * SLICES + c + 1]
-            if c % 2 == 0:
-                nc.scalar.activation(res[:], acc[c][:], ACT.Identity, bias=bias)
-            else:
-                nc.vector.tensor_scalar_add(res[:], acc[c][:], bias)
-            nc.sync.dma_start(out[c * P : (c + 1) * P, :], res[:])
+        a2_right = keep.tile([P, PACK, HALF], F32, name="a2_right", tag="first_then_a2", align_bytes=64)
+        kept_pairs(a2_right, PACK, HALF, KEPT)
+        kept_pairs(a2_left, last, 0, HALF)
+        weave(nc.scalar.copy, halves[0][:], a2_left[:])
+        for u in range(PACK + 1, SLICES):
+            kept_pairs(a2_right, u, HALF, KEPT)
+        quantize(a2_codes[:, KEPT : KEPT + HALF], a2_scales[:, KEPT : KEPT + HALF], halves[0])
+        second_stage(1, 0)
+        weave(nc.vector.tensor_copy, halves[1][:], a2_right[:])
+        finish(0, ())
+        quantize(a2_codes[:, KEPT + HALF :], a2_scales[:, KEPT + HALF :], halves[1])
+        second_stage(1, 1)
+        finish(1, (1,))

@@ -34,7 +34,6 @@ def tile_list_juror_pair_leanings_kernel(
     with ExitStack() as ctx:
         keep = ctx.enter_context(tc.tile_pool(name="keep", bufs=1))
         two = ctx.enter_context(tc.tile_pool(name="two", bufs=2))
-        three = ctx.enter_context(tc.tile_pool(name="three", bufs=3))
         four = ctx.enter_context(tc.tile_pool(name="four", bufs=4))
         ps_h = ctx.enter_context(tc.psum_pool(name="ps_h", bufs=4))
         ps_o = ctx.enter_context(tc.psum_pool(name="ps_o", bufs=1))
@@ -44,7 +43,7 @@ def tile_list_juror_pair_leanings_kernel(
         offs_sb = keep.tile([P, S // 16], U16, name="offs_sb")
         nc.sync.dma_start(offs_sb[:], offs)
         tscale = keep.tile([P, T], U8, name="tscale", align_bytes=64)
-        nc.sync.dma_start(tscale[96:128, :].bitcast(I32), tab_scales.rearrange("a q t -> (a q) t").bitcast(I32))
+        nc.scalar.dma_start(tscale[96:128, :].bitcast(I32), tab_scales.rearrange("a q t -> (a q) t").bitcast(I32))
         nc.vector.memset(tscale[0:96, :].bitcast(I32), 0)
         planes = keep.tile([P, PASSES * S], U8, name="planes", align_bytes=64)
         nc.vector.memset(planes[:].bitcast(I32), 0)
@@ -54,11 +53,11 @@ def tile_list_juror_pair_leanings_kernel(
         w4_raw = keep.tile([P, PASSES, 2 * H // 4], I32, name="w4_raw", align_bytes=64)
         nc.sync.dma_start(w4_raw[:], w4_words.rearrange("a p c -> p a c").bitcast(I32))
         for first, vec in ((ROW0, b1), (ROW0 + SLICES, gain)):
-            nc.sync.dma_start(
+            nc.scalar.dma_start(
                 rows[first : first + SLICES, :].rearrange("u (g i) -> u g i", i=8),
                 vec.rearrange("(g u i) -> u g i", u=SLICES, i=8),
             )
-        nc.sync.dma_start(rows[ROW0 + 2 * SLICES :, :], b2.rearrange("(c p) -> c p", p=P))
+        nc.scalar.dma_start(rows[ROW0 + 2 * SLICES :, :], b2.rearrange("(c p) -> c p", p=P))
 
         def load_list(name, lst, n):
             lst_sb = keep.tile([P, n // 16], U16, name=name)
@@ -91,7 +90,7 @@ def tile_list_juror_pair_leanings_kernel(
         for a in range(PASSES):
             for q in range(4):
                 src = 96 + 16 * a + 4 * q
-                nc.scalar.dma_start(
+                (nc.scalar, nc.sync)[a].dma_start(
                     planes[32 * q : 32 * q + 4, a * S : (a + 1) * S].bitcast(I32), gscale[src : src + 4, :].bitcast(I32)
                 )
         codes = [keep.tile([P, S], U32, name="codes%d" % a, align_bytes=64) for a in range(PASSES)]
@@ -123,7 +122,7 @@ def tile_list_juror_pair_leanings_kernel(
             nc.sync.dma_start(w2_raw[:, u, :], w2_rows[u])
 
         def first_stage(u):
-            h = three.tile([P, S], F32, name="h")
+            h = keep.tile([P, S], F32, name="h%d" % u, tag="h%d" % (u % 3), align_bytes=64)
             cuts = list(range(0, S + 1, BANK))
             if u == 0:
                 cuts.insert(-1, S - BANK // 2)
@@ -155,22 +154,21 @@ def tile_list_juror_pair_leanings_kernel(
             )
 
         w2_woven = [keep.tile([P, N, PACK], BF16, name="w2_woven%d" % b, align_bytes=64) for b in range(PASSES)]
-        w2_codes = keep.tile([P, PASSES * N], U32, name="w2_codes", align_bytes=64)
         w2_scales = keep.tile([P, PASSES * N], U8, name="w2_scales", align_bytes=64)
         a2_pass0 = keep.tile([P, PACK, KEPT], F32, name="a2_pass0", align_bytes=64)
         a2_left = keep.tile([P, PACK, HALF], F32, name="a2_left", align_bytes=64)
-        a2_codes = keep.tile([P, PASSES * KEPT], U32, name="a2_codes", align_bytes=64)
+        a2_codes1 = keep.tile([P, KEPT], U32, name="a2_codes1", align_bytes=64)
         a2_scales = keep.tile([P, PASSES * KEPT], U8, name="a2_scales", align_bytes=64)
         acc = [[ps_o.tile([P, 2, HALF], F32, name="acc%d%d" % (j, cc)) for cc in range(2)] for j in range(2)]
 
-        def second_stage(b, j):
+        def second_stage(w2_codes, a2_codes, b, j):
             for c in range(N // P):
                 lo = b * KEPT + j * HALF
                 nc.tensor.matmul_mx(
                     out=acc[j][c // 2][:, c % 2, :],
                     lhsT=w2_codes[:, b * N + c * P : b * N + (c + 1) * P].bitcast(FP8X4),
                     lhsT_scale=w2_scales[:, b * N + c * P : b * N + (c + 1) * P],
-                    rhs=a2_codes[:, lo : lo + HALF].bitcast(FP8X4),
+                    rhs=a2_codes[:, j * HALF : (j + 1) * HALF].bitcast(FP8X4),
                     rhs_scale=a2_scales[:, lo : lo + HALF],
                     start=(b == 0 and c % 2 == 0),
                     stop=(b == PASSES - 1 and c % 2 == 1),
@@ -191,10 +189,12 @@ def tile_list_juror_pair_leanings_kernel(
                         nc.vector.tensor_scalar_add(res[:, e, :], acc[j][cc][:, e, :], bias)
                     else:
                         nc.scalar.activation(res[:, e, :], acc[j][cc][:, e, :], ACT.Identity, bias=bias)
-                nc.sync.dma_start(
+                queue = nc.scalar if on_vector and cc not in on_vector else nc.sync
+                queue.dma_start(
                     out[2 * cc * P : 2 * (cc + 1) * P, j * HALF : (j + 1) * HALF].rearrange("(e p) n -> p e n", p=P), res[:]
                 )
 
+        last = SLICES - 1
         hs = [first_stage(0), first_stage(1)]
         a1s, factors = [], []
         a2_woven0 = keep.tile([P, KEPT, PACK], BF16, name="a2_woven0", align_bytes=64)
@@ -207,52 +207,53 @@ def tile_list_juror_pair_leanings_kernel(
             factor = four.tile([P, KEPT], F32, name="factor")
             nc.scalar.activation(factor[:], alt_tanh[:], ACT.Copy, scale=cols[:, SLICES + u : SLICES + u + 1])
             factors.append(factor)
-            second = three.tile([P, PAIRS], F32, name="second")
+            second = keep.tile([P, PAIRS], F32, name="second%d" % u, tag="second%d" % (u % 2), align_bytes=64)
             nc.vector.tensor_copy(second[:], h[:].indirect(pos2_sb[:]))
-            first = keep.tile([P, PAIRS], F32, name="first", tag="first_then_a2", align_bytes=64)
             a1 = four.tile([P, PAIRS], F32, name="a1")
-            if u < SLICES - 1:
-                nc.vector.tensor_tensor(first[:], h[:].indirect(pos1_sb[:]), second[:], ALU.subtract)
+            if u < last:
+                excess = keep.tile([P, PAIRS], F32, name="excess", align_bytes=64)
+                nc.vector.tensor_tensor(excess[:], h[:].indirect(pos1_sb[:]), second[:], ALU.subtract)
             else:
+                first = keep.tile([P, PAIRS], F32, name="first", tag="h0", align_bytes=64)
                 nc.vector.tensor_copy(first[:], h[:].indirect(pos1_sb[:]))
             if u + 2 < SLICES:
                 hs.append(first_stage(u + 2))
-            if u < SLICES - 1:
-                excess = two.tile([P, PAIRS], F32, name="excess")
-                nc.scalar.activation(excess[:], first[:], ACT.Relu)
+            if u < last:
+                nc.scalar.activation(excess[:], excess[:], ACT.Relu)
                 nc.gpsimd.tensor_tensor(a1[:], excess[:], second[:], ALU.add)
-            if u > 0:
-                if u - 1 < PACK:
-                    kept_pairs(a2_pass0, u - 1, 0, KEPT)
-                else:
-                    kept_pairs(a2_left, u - 1, 0, HALF)
-            if u == SLICES - 1:
+            if u == last - 2:
+                w2_codes = keep.tile([P, PASSES * N], U32, name="w2_codes", tag="h2", align_bytes=64)
+                for b in range(PASSES):
+                    quantize(w2_codes[:, b * N : (b + 1) * N], w2_scales[:, b * N : (b + 1) * N], w2_woven[b])
+            if 0 < u <= PACK:
+                kept_pairs(a2_pass0, u - 1, 0, KEPT)
+            elif u > PACK:
+                kept_pairs(a2_left, u - 1, 0, HALF)
+            if u == last:
                 nc.vector.tensor_tensor(a1[:], first[:], second[:], ALU.max)
             a1s.append(a1)
             if u < 2 * PASSES:
                 b, lo = u // 2, (u % 2) * HALF
                 weave(nc.scalar.copy, w2_woven[b][:, lo : lo + HALF, :], w2_raw[:, b * PACK : (b + 1) * PACK, lo : lo + HALF])
-            if u == PACK:
-                weave(nc.scalar.copy, a2_woven0[:], a2_pass0[:])
-                for b in range(PASSES):
-                    quantize(w2_codes[:, b * N : (b + 1) * N], w2_scales[:, b * N : (b + 1) * N], w2_woven[b])
-            if u == PACK + 1:
-                quantize(a2_codes[:, 0:KEPT], a2_scales[:, 0:KEPT], a2_woven0)
-                for j in range(2):
-                    second_stage(0, j)
+            elif u < 2 * PASSES + 2:
+                lo = (u % 2) * HALF
+                weave(nc.scalar.copy, a2_woven0[:, lo : lo + HALF, :], a2_pass0[:, :, lo : lo + HALF])
 
         halves = [keep.tile([P, HALF, PACK], BF16, name="a2_half%d" % j, align_bytes=64) for j in range(2)]
-        last = SLICES - 1
-        a2_right = keep.tile([P, PACK, HALF], F32, name="a2_right", tag="first_then_a2", align_bytes=64)
-        kept_pairs(a2_right, PACK, HALF, KEPT)
+        a2_codes0 = keep.tile([P, KEPT], U32, name="a2_codes0", tag="h0", align_bytes=64)
+        a2_right = keep.tile([P, PACK, HALF], F32, name="a2_right", tag="second1", align_bytes=64)
+        quantize(a2_codes0[:], a2_scales[:, 0:KEPT], a2_woven0)
+        for j in range(2):
+            second_stage(w2_codes, a2_codes0, 0, j)
         kept_pairs(a2_left, last, 0, HALF)
         weave(nc.scalar.copy, halves[0][:], a2_left[:])
-        for u in range(PACK + 1, SLICES):
+        for u in range(PACK, SLICES):
             kept_pairs(a2_right, u, HALF, KEPT)
-        quantize(a2_codes[:, KEPT : KEPT + HALF], a2_scales[:, KEPT : KEPT + HALF], halves[0])
-        second_stage(1, 0)
-        weave(nc.vector.tensor_copy, halves[1][:], a2_right[:])
+        quantize(a2_codes1[:, 0:HALF], a2_scales[:, KEPT : KEPT + HALF], halves[0])
+        second_stage(w2_codes, a2_codes1, 1, 0)
+        weave(nc.scalar.copy, halves[1][:, 0 : HALF // 2, :], a2_right[:, :, 0 : HALF // 2])
+        weave(nc.vector.tensor_copy, halves[1][:, HALF // 2 :, :], a2_right[:, :, HALF // 2 :])
         finish(0, ())
-        quantize(a2_codes[:, KEPT + HALF :], a2_scales[:, KEPT + HALF :], halves[1])
-        second_stage(1, 1)
+        quantize(a2_codes1[:, HALF:], a2_scales[:, KEPT + HALF :], halves[1])
+        second_stage(w2_codes, a2_codes1, 1, 1)
         finish(1, (1,))

from contextlib import ExitStack

import concourse.mybir as mybir
from concourse.masks import make_identity

K, H, N, T, S, PAIRS, KEPT = 1024, 1024, 512, 4096, 2048, 1024, 512
FLOPS = 2 * K * H * S + 2 * H * N * KEPT

F32 = mybir.dt.float32
BF16 = mybir.dt.bfloat16
I32 = mybir.dt.int32
U32 = mybir.dt.uint32
U16 = mybir.dt.uint16
U8 = mybir.dt.uint8
FP8X4 = mybir.dt.float8_e4m3fn_x4
FP4X4 = mybir.dt.float4_e2m1fn_x4
ACT = mybir.ActivationFunctionType
ALU = mybir.AluOpType

P = 128
PASSES = 2
PACK = 4
SLICES = 8
BANK = 512
CHUNKS = S // BANK
HALF = KEPT // 2
ROW0 = P - (2 * SLICES + N // P)


def tile_list_juror_pair_leanings_kernel(
    tc, tab_words, tab_scales, offs, pos1, pos2, pos3, pos4, w4_words, w4_scales, b1, gain, w2, b2, out
):
    nc = tc.nc
    with ExitStack() as ctx:
        keep = ctx.enter_context(tc.tile_pool(name="keep", bufs=1))
        two = ctx.enter_context(tc.tile_pool(name="two", bufs=2))
        four = ctx.enter_context(tc.tile_pool(name="four", bufs=4))
        ps_h = ctx.enter_context(tc.psum_pool(name="ps_h", bufs=4))
        ps_o = ctx.enter_context(tc.psum_pool(name="ps_o", bufs=1))

        rows = keep.tile([P, P], F32, name="rows")
        nc.gpsimd.memset(rows[0:ROW0, :], 0.0)
        offs_sb = keep.tile([P, S // 16], U16, name="offs_sb")
        nc.sync.dma_start(offs_sb[:], offs)
        tscale = keep.tile([P, T], U8, name="tscale", align_bytes=64)
        nc.scalar.dma_start(tscale[96:128, :].bitcast(I32), tab_scales.rearrange("a q t -> (a q) t").bitcast(I32))
        nc.vector.memset(tscale[0:96, :].bitcast(I32), 0)
        planes = keep.tile([P, PASSES * S], U8, name="planes", align_bytes=64)
        nc.vector.memset(planes[:].bitcast(I32), 0)

        tab0 = keep.tile([P, T], I32, name="tab0", align_bytes=64)
        nc.sync.dma_start(tab0[:], tab_words[0].rearrange("p n t -> p (n t)").bitcast(I32))
        w4_raw = keep.tile([P, PASSES, 2 * H // 4], I32, name="w4_raw", align_bytes=64)
        nc.sync.dma_start(w4_raw[:], w4_words.rearrange("a p c -> p a c").bitcast(I32))
        for first, vec in ((ROW0, b1), (ROW0 + SLICES, gain)):
            nc.scalar.dma_start(
                rows[first : first + SLICES, :].rearrange("u (g i) -> u g i", i=8),
                vec.rearrange("(g u i) -> u g i", u=SLICES, i=8),
            )
        nc.scalar.dma_start(rows[ROW0 + 2 * SLICES :, :], b2.rearrange("(c p) -> c p", p=P))

        def load_list(name, lst, n):
            lst_sb = keep.tile([P, n // 16], U16, name=name)
            nc.sync.dma_start(lst_sb[:], lst)
            return lst_sb

        pos4_sb = load_list("pos4_sb", pos4, KEPT)
        tab1 = keep.tile([P, T], I32, name="tab1", tag="tab1_then_w2", align_bytes=64)
        nc.sync.dma_start(tab1[:], tab_words[1].rearrange("p n t -> p (n t)").bitcast(I32))
        tab = (tab0, tab1)
        pos2_sb = load_list("pos2_sb", pos2, PAIRS)
        pos1_sb = load_list("pos1_sb", pos1, PAIRS)
        pos3_sb = load_list("pos3_sb", pos3, KEPT)

        w4s_raw = keep.tile([P, PASSES, H // 4], I32, name="w4s_raw", align_bytes=64)
        nc.gpsimd.memset(w4s_raw[:], 0)
        for q in range(4):
            nc.gpsimd.dma_start(
                w4s_raw[32 * q : 32 * q + 4, :, :],
                w4_scales[:, 4 * q : 4 * q + 4, :].rearrange("a r c -> r a c").bitcast(I32),
            )
        ident = keep.tile([P, P], F32, name="ident")
        make_identity(nc, ident[:])
        cols_ps = ps_h.tile([P, P], F32, name="cols_ps", tag="bank")
        nc.tensor.transpose(cols_ps[:], rows[:], ident[:])
        cols = keep.tile([P, 2 * SLICES + 4], F32, name="cols")

        gscale = keep.tile([P, S], U8, name="gscale", align_bytes=64)
        nc.vector.tensor_copy(gscale[:], tscale[:].indirect(offs_sb[:]))
        for a in range(PASSES):
            for q in range(4):
                src = 96 + 16 * a + 4 * q
                (nc.scalar, nc.sync)[a].dma_start(
                    planes[32 * q : 32 * q + 4, a * S : (a + 1) * S].bitcast(I32), gscale[src : src + 4, :].bitcast(I32)
                )
        codes = [keep.tile([P, S], U32, name="codes%d" % a, align_bytes=64) for a in range(PASSES)]

        def gather_words(a, lo, hi):
            nc.vector.tensor_copy(codes[a][:, lo:hi], tab[a][:].bitcast(U32).indirect(offs_sb[:, lo // 16 : hi // 16]))

        for c in range(CHUNKS):
            gather_words(0, c * BANK, (c + 1) * BANK)

        nc.vector.tensor_copy(cols[:], cols_ps[:, ROW0:])
        w4 = keep.tile([P, PASSES * 2 * H], U8, name="w4", align_bytes=64)
        w4s = keep.tile([P, PASSES * H], U8, name="w4s", align_bytes=64)
        for a in range(PASSES):
            nc.gpsimd.tensor_copy(
                w4s[:, a * H : (a + 1) * H].bitcast(I32).rearrange("p (u g w) -> p u g w", u=SLICES, w=2),
                w4s_raw[:, a, :].rearrange("p (g u w) -> p u g w", u=SLICES, w=2),
            )
            nc.gpsimd.tensor_copy(
                w4[:, a * 2 * H : (a + 1) * 2 * H].bitcast(I32).rearrange("p (u g w) -> p u g w", u=SLICES, w=4),
                w4_raw[:, a, :].rearrange("p (g u w) -> p u g w", u=SLICES, w=4),
            )
        for c in range(CHUNKS):
            gather_words(1, c * BANK, (c + 1) * BANK)

        w2_raw = keep.tile([P, SLICES, N], F32, name="w2_raw", tag="tab1_then_w2", align_bytes=64)
        w2_rows = w2.rearrange("(g u i) n -> u g i n", u=SLICES, i=8)
        for u in range(SLICES):
            nc.sync.dma_start(w2_raw[:, u, :], w2_rows[u])

        def first_stage(u):
            h = keep.tile([P, S], F32, name="h%d" % u, tag="h%d" % (u % 3), align_bytes=64)
            cuts = list(range(0, S + 1, BANK))
            if u == 0:
                cuts.insert(-1, S - BANK // 2)
            for lo, hi in zip(cuts, cuts[1:]):
                bank = ps_h.tile([P, hi - lo], F32, name="bank", tag="bank")
                for a in range(PASSES):
                    col = (a * SLICES + u) * P
                    nc.tensor.matmul_mx(
                        out=bank[:],
                        lhsT=w4[:, 2 * col : 2 * (col + P)].bitcast(FP4X4),
                        lhsT_scale=w4s[:, col : col + P],
                        rhs=codes[a][:, lo:hi].bitcast(FP8X4),
                        rhs_scale=planes[:, a * S + lo : a * S + hi],
                        start=(a == 0),
                        stop=(a == PASSES - 1),
                    )
                nc.scalar.activation(h[:, lo:hi], bank[:], ACT.Gelu_apprx_tanh, bias=cols[:, u : u + 1])
            return h

        def weave(copy, dst, src):
            copy(
                dst.rearrange("p (c i) t -> p c t i", i=4),
                src.rearrange("p t (c i) -> p c t i", i=4),
            )

        def quantize(codes_ap, scales_ap, woven):
            nc.vector.quantize_mx(
                out=codes_ap.bitcast(FP8X4), scales=scales_ap, in_=woven[:].rearrange("p c t -> p (c t)")
            )

        w2_woven = [keep.tile([P, N, PACK], BF16, name="w2_woven%d" % b, align_bytes=64) for b in range(PASSES)]
        w2_scales = keep.tile([P, PASSES * N], U8, name="w2_scales", align_bytes=64)
        a2_pass0 = keep.tile([P, PACK, KEPT], F32, name="a2_pass0", align_bytes=64)
        a2_left = keep.tile([P, PACK, HALF], F32, name="a2_left", align_bytes=64)
        a2_codes1 = keep.tile([P, KEPT], U32, name="a2_codes1", align_bytes=64)
        a2_scales = keep.tile([P, PASSES * KEPT], U8, name="a2_scales", align_bytes=64)
        acc = [[ps_o.tile([P, 2, HALF], F32, name="acc%d%d" % (j, cc)) for cc in range(2)] for j in range(2)]

        def second_stage(w2_codes, a2_codes, b, j):
            for c in range(N // P):
                lo = b * KEPT + j * HALF
                nc.tensor.matmul_mx(
                    out=acc[j][c // 2][:, c % 2, :],
                    lhsT=w2_codes[:, b * N + c * P : b * N + (c + 1) * P].bitcast(FP8X4),
                    lhsT_scale=w2_scales[:, b * N + c * P : b * N + (c + 1) * P],
                    rhs=a2_codes[:, j * HALF : (j + 1) * HALF].bitcast(FP8X4),
                    rhs_scale=a2_scales[:, lo : lo + HALF],
                    start=(b == 0 and c % 2 == 0),
                    stop=(b == PASSES - 1 and c % 2 == 1),
                )

        def kept_pairs(dst, u, lo, hi):
            nc.vector.tensor_tensor(
                dst[:, u % PACK, :], a1s[u][:].indirect(pos3_sb[:, lo // 16 : hi // 16]), factors[u][:, lo:hi], ALU.mult
            )

        def finish(j, on_vector):
            for cc in range(2):
                res = keep.tile([P, 2, HALF], F32, name="res%d%d" % (j, cc))
                for e in range(2):
                    c = 2 * cc + e
                    bias = cols[:, 2 * SLICES + c : 2 * SLICES + c + 1]
                    if cc in on_vector:
                        nc.vector.tensor_scalar_add(res[:, e, :], acc[j][cc][:, e, :], bias)
                    else:
                        nc.scalar.activation(res[:, e, :], acc[j][cc][:, e, :], ACT.Identity, bias=bias)
                queue = nc.scalar if on_vector and cc not in on_vector else nc.sync
                queue.dma_start(
                    out[2 * cc * P : 2 * (cc + 1) * P, j * HALF : (j + 1) * HALF].rearrange("(e p) n -> p e n", p=P), res[:]
                )

        last = SLICES - 1
        hs = [first_stage(0), first_stage(1)]
        a1s, factors = [], []
        a2_woven0 = keep.tile([P, KEPT, PACK], BF16, name="a2_woven0", align_bytes=64)
        for u in range(SLICES):
            h = hs[u]
            alt = two.tile([P, KEPT], F32, name="alt")
            nc.vector.tensor_copy(alt[:], h[:].indirect(pos4_sb[:]))
            alt_tanh = two.tile([P, KEPT], F32, name="alt_tanh")
            nc.scalar.activation(alt_tanh[:], alt[:], ACT.Tanh)
            factor = four.tile([P, KEPT], F32, name="factor")
            nc.scalar.activation(factor[:], alt_tanh[:], ACT.Copy, scale=cols[:, SLICES + u : SLICES + u + 1])
            factors.append(factor)
            second = keep.tile([P, PAIRS], F32, name="second%d" % u, tag="second%d" % (u % 2), align_bytes=64)
            nc.vector.tensor_copy(second[:], h[:].indirect(pos2_sb[:]))
            a1 = four.tile([P, PAIRS], F32, name="a1")
            if u < last:
                excess = keep.tile([P, PAIRS], F32, name="excess", align_bytes=64)
                nc.vector.tensor_tensor(excess[:], h[:].indirect(pos1_sb[:]), second[:], ALU.subtract)
            else:
                first = keep.tile([P, PAIRS], F32, name="first", tag="h0", align_bytes=64)
                nc.vector.tensor_copy(first[:], h[:].indirect(pos1_sb[:]))
            if u + 2 < SLICES:
                hs.append(first_stage(u + 2))
            if u < last:
                nc.scalar.activation(excess[:], excess[:], ACT.Relu)
                nc.gpsimd.tensor_tensor(a1[:], excess[:], second[:], ALU.add)
            if u == last - 2:
                w2_codes = keep.tile([P, PASSES * N], U32, name="w2_codes", tag="h2", align_bytes=64)
                for b in range(PASSES):
                    quantize(w2_codes[:, b * N : (b + 1) * N], w2_scales[:, b * N : (b + 1) * N], w2_woven[b])
            if 0 < u <= PACK:
                kept_pairs(a2_pass0, u - 1, 0, KEPT)
            elif u > PACK:
                kept_pairs(a2_left, u - 1, 0, HALF)
            if u == last:
                nc.vector.tensor_tensor(a1[:], first[:], second[:], ALU.max)
            a1s.append(a1)
            if u < 2 * PASSES:
                b, lo = u // 2, (u % 2) * HALF
                weave(nc.scalar.copy, w2_woven[b][:, lo : lo + HALF, :], w2_raw[:, b * PACK : (b + 1) * PACK, lo : lo + HALF])
            elif u < 2 * PASSES + 2:
                lo = (u % 2) * HALF
                weave(nc.scalar.copy, a2_woven0[:, lo : lo + HALF, :], a2_pass0[:, :, lo : lo + HALF])

        halves = [keep.tile([P, HALF, PACK], BF16, name="a2_half%d" % j, align_bytes=64) for j in range(2)]
        a2_codes0 = keep.tile([P, KEPT], U32, name="a2_codes0", tag="h0", align_bytes=64)
        a2_right = keep.tile([P, PACK, HALF], F32, name="a2_right", tag="second1", align_bytes=64)
        quantize(a2_codes0[:], a2_scales[:, 0:KEPT], a2_woven0)
        for j in range(2):
            second_stage(w2_codes, a2_codes0, 0, j)
        kept_pairs(a2_left, last, 0, HALF)
        weave(nc.scalar.copy, halves[0][:], a2_left[:])
        for u in range(PACK, SLICES):
            kept_pairs(a2_right, u, HALF, KEPT)
        quantize(a2_codes1[:, 0:HALF], a2_scales[:, KEPT : KEPT + HALF], halves[0])
        second_stage(w2_codes, a2_codes1, 1, 0)
        weave(nc.scalar.copy, halves[1][:, 0 : HALF // 2, :], a2_right[:, :, 0 : HALF // 2])
        weave(nc.vector.tensor_copy, halves[1][:, HALF // 2 :, :], a2_right[:, :, HALF // 2 :])
        finish(0, ())
        quantize(a2_codes1[:, HALF:], a2_scales[:, KEPT + HALF :], halves[1])
        second_stage(w2_codes, a2_codes1, 1, 1)
        finish(1, (1,))
